import numpy as np
import ml_dtypes


def mxq(x, axis, fmt="e4m3"):
    dtype, down = {"e4m3": (ml_dtypes.float8_e4m3fn, 7), "e5m2": (ml_dtypes.float8_e5m2, 14)}[fmt]
    v = np.moveaxis(np.asarray(x, np.float32).astype(ml_dtypes.bfloat16).astype(np.float64), axis, -1)
    blocks = v.reshape(v.shape[:-1] + (-1, 32))
    amax = np.abs(blocks).max(-1, keepdims=True)
    byte = np.maximum(np.where(amax > 0, np.frexp(amax)[1] - 1 + 127, 0) - down, 1)
    scale = np.exp2(byte - 127.0)
    codes = (blocks / scale).astype(np.float32).astype(dtype).astype(np.float64)
    return np.moveaxis((codes * scale).reshape(v.shape), -1, axis)


WIDE = False


def mx_kscale(k):
    if not WIDE:
        return np.ones(k)
    levels = np.array([10, -10, 5, -5, 0])
    if k % 512:
        return np.exp2(np.random.permutation(np.resize(levels, k // 32))).repeat(32)
    a = np.empty((k // 512, 16))
    for p in range(k // 512):
        a[p, :8] = np.random.permutation(np.resize(levels, 8))
        for g in range(8):
            far = levels[np.abs(levels - a[p, g]) >= 10]
            a[p, g + 8] = far[np.random.randint(len(far))]
    return np.exp2(a.ravel()).repeat(32)


def f64(x):
    return np.asarray(x).astype(np.float64)


def striped(idx):
    return np.tile(np.asarray(idx).reshape(-1, 16).T, (8, 1)).astype(np.uint16)


def unstriped(offs):
    return offs[:16].T.reshape(-1).astype(np.int64)


E2M1 = np.array([0.0, 0.5, 1.0, 1.5, 2.0, 3.0, 4.0, 6.0, -0.0, -0.5, -1.0, -1.5, -2.0, -3.0, -4.0, -6.0])


def pack_weight(w, fmt):
    k, n = w.shape
    w = f64(np.asarray(w, np.float32).astype(ml_dtypes.bfloat16)).reshape(k // 32, 32, n)
    amax = np.abs(w).max(1)
    if fmt == "e4m3":
        byte = np.frexp(amax)[1] - 1 + 127 - 7
    else:
        mant, ex = np.frexp(amax / 6.0)
        byte = np.where(mant > 0.5, ex, ex - 1) + 127
    byte = np.clip(np.where(amax > 0, byte, 1), 1, 254)
    scaled = (w * np.exp2(127.0 - byte)[:, None, :]).reshape(k, n).astype(np.float32)
    by_word = np.ascontiguousarray(scaled.reshape(k // 512, 128, 4, n).transpose(0, 1, 3, 2))
    if fmt == "e4m3":
        words = by_word.astype(ml_dtypes.float8_e4m3fn).view(np.uint8)
    else:
        c = by_word.astype(ml_dtypes.float4_e2m1fn).view(np.uint8) & 0xF
        words = (c[..., 0::2] | (c[..., 1::2] << 4)).reshape(k // 512, 128, 2 * n)
    return np.ascontiguousarray(words), np.ascontiguousarray(byte.astype(np.uint8).reshape(k // 512, 16, n))


def unpack_weight(words, scales, fmt):
    g, _, n = scales.shape
    words = np.ascontiguousarray(words).reshape(g, 128, n, -1)
    if fmt == "e4m3":
        vals = words.view(ml_dtypes.float8_e4m3fn).astype(np.float64)
    else:
        nib = np.empty((g, 128, n, 4), np.uint8)
        nib[..., 0::2] = words & 0xF
        nib[..., 1::2] = words >> 4
        vals = E2M1[nib]
    vals = vals * np.repeat(np.exp2(scales.astype(np.float64) - 127.0), 8, axis=1)[..., None]
    return vals.transpose(0, 1, 3, 2).reshape(g * 512, n)


K, L, T, C, J = 512, 1024, 256, 1024, 512


def setup_inputs():
    n = np.random.standard_normal
    idx = np.random.permutation(C)[:J]
    fk = mx_kscale(K)
    fl = mx_kscale(L)
    xtp = pack_weight(n((K, T)) * 0.5 / fk[:, None], "e4m3")
    xlp = pack_weight(n((L, T)) * 0.5 / fl[:, None], "e2m1")
    wlp = pack_weight(n((L, C)) * 1 / np.sqrt(L) * fl[:, None], "e4m3")
    return {
        "xt_words": xtp[0],
        "xt_scales": xtp[1],
        "wc": (n((K, J)) * 1 / np.sqrt(K) * fk[:, None]).astype(np.float32),
        "xl_words": xlp[0],
        "xl_scales": xlp[1],
        "wl_words": wlp[0],
        "wl_scales": wlp[1],
        "offs": striped(idx),
    }


def reference(xt_words, xt_scales, wc, xl_words, xl_scales, wl_words, wl_scales, offs):
    idx = unstriped(offs)
    xtu = unpack_weight(xt_words, xt_scales, "e4m3")
    xlu = unpack_weight(xl_words, xl_scales, "e2m1")
    wlu = unpack_weight(wl_words, wl_scales, "e4m3")
    wcq = mxq(f64(wc), 0, "e4m3")
    z = xtu.T @ wcq
    u = xlu.T @ wlu
    p = np.exp(z)
    q = np.exp(u[:, idx])
    y = 256.0 * p / np.sum(p, axis=1, keepdims=True) - 256.0 * q / np.sum(q, axis=1, keepdims=True)
    return y

@@ -1,0 +1,146 @@
+from contextlib import ExitStack
+
+import concourse.mybir as mybir
+
+K, L, T, C, J = 512, 1024, 256, 1024, 512
+FLOPS = 2 * T * (K * J + L * C)
+
+F32 = mybir.dt.float32
+BF16 = mybir.dt.bfloat16
+I32 = mybir.dt.int32
+U32 = mybir.dt.uint32
+U16 = mybir.dt.uint16
+U8 = mybir.dt.uint8
+FP8X4 = mybir.dt.float8_e4m3fn_x4
+FP4X4 = mybir.dt.float4_e2m1fn_x4
+ALU = mybir.AluOpType
+ACT = mybir.ActivationFunctionType
+AX = mybir.AxisListType
+
+P = 128
+HALF = 256
+VCOLS = 176
+
+
+def tile_list_teacher_at_listed_classes_kernel(tc, xt_words, xt_scales, wc, xl_words, xl_scales, wl_words, wl_scales, offs, out):
+    nc = tc.nc
+    with ExitStack() as ctx:
+        lists = ctx.enter_context(tc.tile_pool(name="lists", bufs=1))
+        keep = ctx.enter_context(tc.tile_pool(name="keep", bufs=1))
+        psum = ctx.enter_context(tc.psum_pool(name="psum", bufs=1))
+
+        offsets = lists.tile([P, J // 16], U16, name="offsets")
+        xt_w = keep.tile([P, T], U32, name="xt_w", align_bytes=64)
+        xl_w = keep.tile([P, 2, 2 * T], U8, name="xl_w", align_bytes=64)
+        wl_w = [keep.tile([P, 2, 512], U32, name="wl_w%d" % h, align_bytes=64) for h in range(2)]
+        xt_s = keep.tile([P, 1, T], U8, name="xt_s", align_bytes=64)
+        xl_s = keep.tile([P, 2, T], U8, name="xl_s", align_bytes=64)
+        wl_s = keep.tile([P, 2, C], U8, name="wl_s", align_bytes=64)
+        raw = [keep.tile([P, 4, HALF], F32, name="raw%d" % h) for h in range(2)]
+        grouped = [keep.tile([P, HALF, 4], BF16, name="grouped%d" % h, align_bytes=64) for h in range(2)]
+        wc_w = [keep.tile([P, HALF], U32, name="wc_w%d" % h, align_bytes=64) for h in range(2)]
+        wc_s = [keep.tile([P, HALF], U8, name="wc_s%d" % h, align_bytes=64) for h in range(2)]
+        u_sb = [keep.tile([P, C], F32, name="u_sb%d" % t) for t in range(2)]
+        picked = [keep.tile([P, J], F32, name="picked%d" % t) for t in range(2)]
+        p_exp = [keep.tile([P, J], F32, name="p_exp%d" % t) for t in range(2)]
+        p_share = [keep.tile([P, J], F32, name="p_share%d" % t) for t in range(2)]
+        q_exp = [keep.tile([P, J], F32, name="q_exp%d" % t) for t in range(2)]
+        res = [[keep.tile([P, HALF], F32, name="res%d_%d" % (t, h)) for h in range(2)] for t in range(2)]
+        col = lambda name: [keep.tile([P, 1], F32, name="%s%d" % (name, t)) for t in range(2)]
+        z_max, z_sum, z_rec, q_max, q_sum, q_rec, q_fac = (col(n) for n in ("zm", "zs", "zr", "qm", "qs", "qr", "qf"))
+        z_sums = keep.tile([P, 2], F32, name="z_sums")
+        z_recs = keep.tile([P, 2], F32, name="z_recs")
+        z_facs = keep.tile([P, 2], F32, name="z_facs")
+        z_ps = [psum.tile([P, J], F32, name="z_ps%d" % t) for t in range(2)]
+        u_ps = [[psum.tile([P, 512], F32, name="u_ps%d_%d" % (t, h)) for h in range(2)] for t in range(2)]
+
+        def load_scales(eng, plane, src, quads):
+            for q in quads:
+                eng.dma_start(out=plane[32 * q : 32 * q + 4].bitcast(I32), in_=src[:, 4 * q : 4 * q + 4, :].rearrange("z r n -> r z n").bitcast(I32))
+
+        def load_wc(h):
+            nc.sync.dma_start(out=raw[h][:], in_=wc[:, h * HALF : (h + 1) * HALF].rearrange("(p t) j -> p t j", t=4))
+
+        def load_wl(h):
+            nc.sync.dma_start(out=wl_w[h][:].bitcast(I32), in_=wl_words[:, :, 512 * h : 512 * h + 512, :].rearrange("z p n t -> p z (n t)").bitcast(I32))
+
+        def interleave(h):
+            for eng, a, b in ((nc.vector, 0, HALF),):
+                dst = grouped[h][:, a:b, :].rearrange("p (c i) t -> p c t i", i=4)
+                src = raw[h][:, :, a:b].rearrange("p t (c i) -> p c t i", i=4)
+                if eng is nc.vector:
+                    eng.tensor_copy(out=dst, in_=src)
+                else:
+                    eng.copy(out=dst, in_=src)
+
+        def quantise(h):
+            nc.vector.quantize_mx(out=wc_w[h][:].bitcast(FP8X4), scales=wc_s[h][:], in_=grouped[h][:].rearrange("p c t -> p (c t)"))
+
+        def student_mm(h):
+            for t in range(2):
+                nc.tensor.matmul_mx(out=z_ps[t][:, h * HALF : (h + 1) * HALF], lhsT=xt_w[:, t * P : (t + 1) * P].bitcast(FP8X4), lhsT_scale=xt_s[:, 0, t * P : (t + 1) * P], rhs=wc_w[h][:].bitcast(FP8X4), rhs_scale=wc_s[h][:], start=True, stop=True)
+
+        def teacher_mm(t, h):
+            for z in range(2):
+                nc.tensor.matmul_mx(out=u_ps[t][h][:], lhsT=xl_w[:, z, 2 * t * P : 2 * (t + 1) * P].bitcast(FP4X4), lhsT_scale=xl_s[:, z, t * P : (t + 1) * P], rhs=wl_w[h][:, z, :].bitcast(FP8X4), rhs_scale=wl_s[:, z, 512 * h : 512 * h + 512], start=(z == 0), stop=(z == 1))
+
+        def evac(t, h):
+            nc.scalar.activation(out=u_sb[t][:, 512 * h : 512 * h + 512], in_=u_ps[t][h][:], func=ACT.Copy)
+
+        def neg_max(dst, src):
+            nc.vector.tensor_reduce(out=dst[:], in_=src, axis=AX.X, op=ALU.max, negate=True)
+
+        def gather(t):
+            nc.vector.tensor_copy(out=picked[t][:], in_=u_sb[t][:].indirect(offsets[:]))
+
+        def q_finish(t, engs):
+            nc.vector.reciprocal(out=q_rec[t][:], in_=q_sum[t][:])
+            nc.vector.tensor_scalar(out=q_fac[t][:], in0=q_rec[t][:], scalar1=-256.0, scalar2=None, op0=ALU.mult)
+            for h in range(2):
+                cols = slice(h * HALF, (h + 1) * HALF)
+                nc.vector.scalar_tensor_tensor(out=res[t][h][:], in0=q_exp[t][:, cols], scalar=q_fac[t][:], in1=p_share[t][:, cols], op0=ALU.mult, op1=ALU.add)
+                engs[h].dma_start(out=out[t * P : (t + 1) * P, cols], in_=res[t][h][:])
+
+        nc.scalar.dma_start(out=xt_w[:].bitcast(I32), in_=xt_words[0].rearrange("p n t -> p (n t)").bitcast(I32))
+        load_scales(nc.gpsimd, xl_s, xl_scales, (0, 1))
+        load_scales(nc.scalar, xt_s, xt_scales, range(4))
+        load_scales(nc.scalar, wl_s, wl_scales, (0,))
+        load_wc(0)
+        load_wc(1)
+        load_scales(nc.scalar, wl_s, wl_scales, (1, 2))
+        load_wl(0)
+        nc.sync.dma_start(out=xl_w[:].bitcast(I32), in_=xl_words.rearrange("z p b -> p z b").bitcast(I32))
+        load_scales(nc.scalar, wl_s, wl_scales, (3,))
+        load_scales(nc.scalar, xl_s, xl_scales, (2,))
+        load_wl(1)
+        nc.sync.dma_start(offsets[:], offs)
+        load_scales(nc.scalar, xl_s, xl_scales, (3,))
+        interleave(0)
+        quantise(0)
+        interleave(1)
+        quantise(1)
+        student_mm(0)
+        student_mm(1)
+        teacher_mm(0, 0)
+        teacher_mm(0, 1)
+        teacher_mm(1, 0)
+        teacher_mm(1, 1)
+        for t in range(2):
+            neg_max(z_max[t], z_ps[t][:])
+        evac(0, 0)
+        evac(0, 1)
+        evac(1, 0)
+        evac(1, 1)
+        gather(0)
+        gather(1)
+        for t in range(2):
+            neg_max(q_max[t], picked[t][:])
+            nc.scalar.activation(out=q_exp[t][:], in_=picked[t][:], func=ACT.Exp, bias=q_max[t][:], accum_out=q_sum[t][:])
+        for t in range(2):
+            nc.scalar.activation(out=p_exp[t][:], in_=z_ps[t][:], func=ACT.Exp, bias=z_max[t][:], accum_out=z_sums[:, t : t + 1])
+        nc.vector.reciprocal(out=z_recs[:], in_=z_sums[:])
+        nc.vector.tensor_scalar(out=z_facs[:], in0=z_recs[:], scalar1=256.0, scalar2=None, op0=ALU.mult)
+        for t in range(2):
+            nc.scalar.activation(out=p_share[t][:], in_=p_exp[t][:], func=ACT.Copy, scale=z_facs[:, t : t + 1])
+        q_finish(0, (nc.sync, nc.sync))
+        q_finish(1, (nc.sync, nc.scalar))

@@ -32,7 +32,9 @@ def tile_list_teacher_at_listed_classes_kernel(tc, xt_words, xt_scales, wc, xl_w
         offsets = lists.tile([P, J // 16], U16, name="offsets")
         xt_w = keep.tile([P, T], U32, name="xt_w", align_bytes=64)
         xl_w = keep.tile([P, 2, 2 * T], U8, name="xl_w", align_bytes=64)
-        wl_w = [keep.tile([P, 2, 512], U32, name="wl_w%d" % h, align_bytes=64) for h in range(2)]
+        wl_a = keep.tile([P, 2, 512], U32, name="wl_a", align_bytes=64)
+        wl_b = [keep.tile([P, 512], U32, name="wl_b%d" % z, align_bytes=64) for z in range(2)]
+        wl_w = [[wl_a[:, 0, :], wl_a[:, 1, :]], [wl_b[0][:], wl_b[1][:]]]
         xt_s = keep.tile([P, 1, T], U8, name="xt_s", align_bytes=64)
         xl_s = keep.tile([P, 2, T], U8, name="xl_s", align_bytes=64)
         wl_s = keep.tile([P, 2, C], U8, name="wl_s", align_bytes=64)
@@ -61,8 +63,11 @@ def tile_list_teacher_at_listed_classes_kernel(tc, xt_words, xt_scales, wc, xl_w
         def load_wc(h):
             nc.sync.dma_start(out=raw[h][:], in_=wc[:, h * HALF : (h + 1) * HALF].rearrange("(p t) j -> p t j", t=4))
 
-        def load_wl(h):
-            nc.sync.dma_start(out=wl_w[h][:].bitcast(I32), in_=wl_words[:, :, 512 * h : 512 * h + 512, :].rearrange("z p n t -> p z (n t)").bitcast(I32))
+        def load_wl_a():
+            nc.sync.dma_start(out=wl_a[:].bitcast(I32), in_=wl_words[:, :, 0:512, :].rearrange("z p n t -> p z (n t)").bitcast(I32))
+
+        def load_wl_b(z):
+            nc.sync.dma_start(out=wl_b[z][:].bitcast(I32), in_=wl_words[z, :, 512:1024, :].rearrange("p n t -> p (n t)").bitcast(I32))
 
         def interleave(h):
             for eng, a, b in ((nc.vector, 0, HALF),):
@@ -82,13 +87,13 @@ def tile_list_teacher_at_listed_classes_kernel(tc, xt_words, xt_scales, wc, xl_w
 
         def teacher_mm(t, h):
             for z in range(2):
-                nc.tensor.matmul_mx(out=u_ps[t][h][:], lhsT=xl_w[:, z, 2 * t * P : 2 * (t + 1) * P].bitcast(FP4X4), lhsT_scale=xl_s[:, z, t * P : (t + 1) * P], rhs=wl_w[h][:, z, :].bitcast(FP8X4), rhs_scale=wl_s[:, z, 512 * h : 512 * h + 512], start=(z == 0), stop=(z == 1))
+                nc.tensor.matmul_mx(out=u_ps[t][h][:], lhsT=xl_w[:, z, 2 * t * P : 2 * (t + 1) * P].bitcast(FP4X4), lhsT_scale=xl_s[:, z, t * P : (t + 1) * P], rhs=wl_w[h][z].bitcast(FP8X4), rhs_scale=wl_s[:, z, 512 * h : 512 * h + 512], start=(z == 0), stop=(z == 1))
 
         def evac(t, h):
             nc.scalar.activation(out=u_sb[t][:, 512 * h : 512 * h + 512], in_=u_ps[t][h][:], func=ACT.Copy)
 
         def neg_max(dst, src):
-            nc.vector.tensor_reduce(out=dst[:], in_=src, axis=AX.X, op=ALU.max, negate=True)
+            nc.vector.tensor_reduce(out=dst, in_=src, axis=AX.X, op=ALU.max, negate=True)
 
         def gather(t):
             nc.vector.tensor_copy(out=picked[t][:], in_=u_sb[t][:].indirect(offsets[:]))
@@ -101,20 +106,22 @@ def tile_list_teacher_at_listed_classes_kernel(tc, xt_words, xt_scales, wc, xl_w
                 nc.vector.scalar_tensor_tensor(out=res[t][h][:], in0=q_exp[t][:, cols], scalar=q_fac[t][:], in1=p_share[t][:, cols], op0=ALU.mult, op1=ALU.add)
                 engs[h].dma_start(out=out[t * P : (t + 1) * P, cols], in_=res[t][h][:])
 
-        nc.scalar.dma_start(out=xt_w[:].bitcast(I32), in_=xt_words[0].rearrange("p n t -> p (n t)").bitcast(I32))
-        load_scales(nc.gpsimd, xl_s, xl_scales, (0, 1))
-        load_scales(nc.scalar, xt_s, xt_scales, range(4))
-        load_scales(nc.scalar, wl_s, wl_scales, (0,))
+        nc.gpsimd.dma_start(out=xt_w[:].bitcast(I32), in_=xt_words[0].rearrange("p n t -> p (n t)").bitcast(I32))
+        load_scales(nc.gpsimd, xl_s, xl_scales, (3,))
+        load_scales(nc.sync, xt_s, xt_scales, (0,))
+        load_scales(nc.scalar, xt_s, xt_scales, (1,))
+        load_scales(nc.sync, xt_s, xt_scales, (2,))
+        load_scales(nc.scalar, xt_s, xt_scales, (3,))
+        load_scales(nc.scalar, wl_s, wl_scales, (0, 1))
         load_wc(0)
         load_wc(1)
-        load_scales(nc.scalar, wl_s, wl_scales, (1, 2))
-        load_wl(0)
-        nc.sync.dma_start(out=xl_w[:].bitcast(I32), in_=xl_words.rearrange("z p b -> p z b").bitcast(I32))
-        load_scales(nc.scalar, wl_s, wl_scales, (3,))
-        load_scales(nc.scalar, xl_s, xl_scales, (2,))
-        load_wl(1)
+        load_scales(nc.scalar, wl_s, wl_scales, (2, 3))
+        load_wl_a()
+        nc.scalar.dma_start(out=xl_w[:].bitcast(I32), in_=xl_words.rearrange("z p b -> p z b").bitcast(I32))
+        load_scales(nc.scalar, xl_s, xl_scales, (0, 1, 2))
+        load_wl_b(0)
+        load_wl_b(1)
         nc.sync.dma_start(offsets[:], offs)
-        load_scales(nc.scalar, xl_s, xl_scales, (3,))
         interleave(0)
         quantise(0)
         interleave(1)
@@ -126,21 +133,23 @@ def tile_list_teacher_at_listed_classes_kernel(tc, xt_words, xt_scales, wc, xl_w
         teacher_mm(1, 0)
         teacher_mm(1, 1)
         for t in range(2):
-            neg_max(z_max[t], z_ps[t][:])
+            neg_max(z_max[t][:], z_ps[t][:])
         evac(0, 0)
         evac(0, 1)
         evac(1, 0)
         evac(1, 1)
-        gather(0)
-        gather(1)
-        for t in range(2):
-            neg_max(q_max[t], picked[t][:])
-            nc.scalar.activation(out=q_exp[t][:], in_=picked[t][:], func=ACT.Exp, bias=q_max[t][:], accum_out=q_sum[t][:])
         for t in range(2):
             nc.scalar.activation(out=p_exp[t][:], in_=z_ps[t][:], func=ACT.Exp, bias=z_max[t][:], accum_out=z_sums[:, t : t + 1])
-        nc.vector.reciprocal(out=z_recs[:], in_=z_sums[:])
-        nc.vector.tensor_scalar(out=z_facs[:], in0=z_recs[:], scalar1=256.0, scalar2=None, op0=ALU.mult)
+        nc.scalar.activation(out=z_recs[:], in_=z_sums[:], func=ACT.Copy, scale=1.0 / 256.0)
+        gather(0)
+        z_fac = u_sb[0][:, 0:2]
+        nc.vector.reciprocal(out=z_fac, in_=z_recs[:])
         for t in range(2):
-            nc.scalar.activation(out=p_share[t][:], in_=p_exp[t][:], func=ACT.Copy, scale=z_facs[:, t : t + 1])
+            nc.scalar.activation(out=p_share[t][:], in_=p_exp[t][:], func=ACT.Copy, scale=z_fac[:, t : t + 1])
+        gather(1)
+        q_neg = [u_sb[1][:, 0:1], q_max[1][:]]
+        for t in range(2):
+            neg_max(q_neg[t], picked[t][:])
+            nc.scalar.activation(out=q_exp[t][:], in_=picked[t][:], func=ACT.Exp, bias=q_neg[t], accum_out=q_sum[t][:])
         q_finish(0, (nc.sync, nc.sync))
         q_finish(1, (nc.sync, nc.scalar))

@@ -32,9 +32,7 @@ def tile_list_teacher_at_listed_classes_kernel(tc, xt_words, xt_scales, wc, xl_w
         offsets = lists.tile([P, J // 16], U16, name="offsets")
         xt_w = keep.tile([P, T], U32, name="xt_w", align_bytes=64)
         xl_w = keep.tile([P, 2, 2 * T], U8, name="xl_w", align_bytes=64)
-        wl_a = keep.tile([P, 2, 512], U32, name="wl_a", align_bytes=64)
-        wl_b = [keep.tile([P, 512], U32, name="wl_b%d" % z, align_bytes=64) for z in range(2)]
-        wl_w = [[wl_a[:, 0, :], wl_a[:, 1, :]], [wl_b[0][:], wl_b[1][:]]]
+        wl_w = [keep.tile([P, 2, 512], U32, name="wl_w%d" % h, align_bytes=64) for h in range(2)]
         xt_s = keep.tile([P, 1, T], U8, name="xt_s", align_bytes=64)
         xl_s = keep.tile([P, 2, T], U8, name="xl_s", align_bytes=64)
         wl_s = keep.tile([P, 2, C], U8, name="wl_s", align_bytes=64)
@@ -63,20 +61,19 @@ def tile_list_teacher_at_listed_classes_kernel(tc, xt_words, xt_scales, wc, xl_w
         def load_wc(h):
             nc.sync.dma_start(out=raw[h][:], in_=wc[:, h * HALF : (h + 1) * HALF].rearrange("(p t) j -> p t j", t=4))
 
-        def load_wl_a():
-            nc.sync.dma_start(out=wl_a[:].bitcast(I32), in_=wl_words[:, :, 0:512, :].rearrange("z p n t -> p z (n t)").bitcast(I32))
+        def load_wl(h):
+            nc.sync.dma_start(out=wl_w[h][:].bitcast(I32), in_=wl_words[:, :, 512 * h : 512 * h + 512, :].rearrange("z p n t -> p z (n t)").bitcast(I32))
 
-        def load_wl_b(z):
-            nc.sync.dma_start(out=wl_b[z][:].bitcast(I32), in_=wl_words[z, :, 512:1024, :].rearrange("p n t -> p (n t)").bitcast(I32))
-
-        def interleave(h):
-            for eng, a, b in ((nc.vector, 0, HALF),):
+        def interleave(h, split):
+            for eng, a, b in ((nc.vector, 0, split), (nc.scalar, split, HALF)):
+                if a == b:
+                    continue
                 dst = grouped[h][:, a:b, :].rearrange("p (c i) t -> p c t i", i=4)
                 src = raw[h][:, :, a:b].rearrange("p t (c i) -> p c t i", i=4)
                 if eng is nc.vector:
                     eng.tensor_copy(out=dst, in_=src)
                 else:
-                    eng.copy(out=dst, in_=src)
+                    eng.activation(out=dst, in_=src, func=ACT.Copy)
 
         def quantise(h):
             nc.vector.quantize_mx(out=wc_w[h][:].bitcast(FP8X4), scales=wc_s[h][:], in_=grouped[h][:].rearrange("p c t -> p (c t)"))
@@ -87,7 +84,7 @@ def tile_list_teacher_at_listed_classes_kernel(tc, xt_words, xt_scales, wc, xl_w
 
         def teacher_mm(t, h):
             for z in range(2):
-                nc.tensor.matmul_mx(out=u_ps[t][h][:], lhsT=xl_w[:, z, 2 * t * P : 2 * (t + 1) * P].bitcast(FP4X4), lhsT_scale=xl_s[:, z, t * P : (t + 1) * P], rhs=wl_w[h][z].bitcast(FP8X4), rhs_scale=wl_s[:, z, 512 * h : 512 * h + 512], start=(z == 0), stop=(z == 1))
+                nc.tensor.matmul_mx(out=u_ps[t][h][:], lhsT=xl_w[:, z, 2 * t * P : 2 * (t + 1) * P].bitcast(FP4X4), lhsT_scale=xl_s[:, z, t * P : (t + 1) * P], rhs=wl_w[h][:, z, :].bitcast(FP8X4), rhs_scale=wl_s[:, z, 512 * h : 512 * h + 512], start=(z == 0), stop=(z == 1))
 
         def evac(t, h):
             nc.scalar.activation(out=u_sb[t][:, 512 * h : 512 * h + 512], in_=u_ps[t][h][:], func=ACT.Copy)
@@ -106,50 +103,54 @@ def tile_list_teacher_at_listed_classes_kernel(tc, xt_words, xt_scales, wc, xl_w
                 nc.vector.scalar_tensor_tensor(out=res[t][h][:], in0=q_exp[t][:, cols], scalar=q_fac[t][:], in1=p_share[t][:, cols], op0=ALU.mult, op1=ALU.add)
                 engs[h].dma_start(out=out[t * P : (t + 1) * P, cols], in_=res[t][h][:])
 
-        nc.gpsimd.dma_start(out=xt_w[:].bitcast(I32), in_=xt_words[0].rearrange("p n t -> p (n t)").bitcast(I32))
-        load_scales(nc.gpsimd, xl_s, xl_scales, (3,))
-        load_scales(nc.sync, xt_s, xt_scales, (0,))
-        load_scales(nc.scalar, xt_s, xt_scales, (1,))
-        load_scales(nc.sync, xt_s, xt_scales, (2,))
-        load_scales(nc.scalar, xt_s, xt_scales, (3,))
+        load_scales(nc.sync, xl_s, xl_scales, (0,))
+        load_scales(nc.scalar, xl_s, xl_scales, (1,))
+        load_scales(nc.sync, xl_s, xl_scales, (2,))
+        load_scales(nc.scalar, xl_s, xl_scales, (3,))
         load_scales(nc.scalar, wl_s, wl_scales, (0, 1))
+        nc.sync.dma_start(out=xl_w[:].bitcast(I32), in_=xl_words.rearrange("z p b -> p z b").bitcast(I32))
+        load_wl(0)
+        load_scales(nc.sync, wl_s, wl_scales, (2, 3))
+        load_wl(1)
+        nc.sync.dma_start(offsets[:], offs)
+        load_scales(nc.scalar, xt_s, xt_scales, (0, 1))
         load_wc(0)
         load_wc(1)
-        load_scales(nc.scalar, wl_s, wl_scales, (2, 3))
-        load_wl_a()
-        nc.scalar.dma_start(out=xl_w[:].bitcast(I32), in_=xl_words.rearrange("z p b -> p z b").bitcast(I32))
-        load_scales(nc.scalar, xl_s, xl_scales, (0, 1, 2))
-        load_wl_b(0)
-        load_wl_b(1)
-        nc.sync.dma_start(offsets[:], offs)
-        interleave(0)
+        load_scales(nc.sync, xt_s, xt_scales, (2, 3))
+        nc.sync.dma_start(out=xt_w[:].bitcast(I32), in_=xt_words[0].rearrange("p n t -> p (n t)").bitcast(I32))
+        u_ps[1][0] = u_ps[0][0]
+        teacher_mm(0, 0)
+        teacher_mm(0, 1)
+        evac(0, 0)
+        evac(0, 1)
+        teacher_mm(1, 0)
+        teacher_mm(1, 1)
+        evac(1, 0)
+        evac(1, 1)
+        interleave(0, HALF)
+        gather(0)
         quantise(0)
-        interleave(1)
+        interleave(1, 0)
+        gather(1)
         quantise(1)
         student_mm(0)
         student_mm(1)
-        teacher_mm(0, 0)
-        teacher_mm(0, 1)
-        teacher_mm(1, 0)
-        teacher_mm(1, 1)
-        for t in range(2):
-            neg_max(z_max[t][:], z_ps[t][:])
-        evac(0, 0)
-        evac(0, 1)
-        evac(1, 0)
-        evac(1, 1)
-        for t in range(2):
-            nc.scalar.activation(out=p_exp[t][:], in_=z_ps[t][:], func=ACT.Exp, bias=z_max[t][:], accum_out=z_sums[:, t : t + 1])
-        nc.scalar.activation(out=z_recs[:], in_=z_sums[:], func=ACT.Copy, scale=1.0 / 256.0)
-        gather(0)
-        z_fac = u_sb[0][:, 0:2]
-        nc.vector.reciprocal(out=z_fac, in_=z_recs[:])
-        for t in range(2):
-            nc.scalar.activation(out=p_share[t][:], in_=p_exp[t][:], func=ACT.Copy, scale=z_fac[:, t : t + 1])
-        gather(1)
-        q_neg = [u_sb[1][:, 0:1], q_max[1][:]]
+        spent = grouped[1][:].rearrange("p c t -> p (c t)").bitcast(F32)
+        q_neg = [spent[:, 8 * t : 8 * t + 1] for t in range(2)]
         for t in range(2):
             neg_max(q_neg[t], picked[t][:])
             nc.scalar.activation(out=q_exp[t][:], in_=picked[t][:], func=ACT.Exp, bias=q_neg[t], accum_out=q_sum[t][:])
-        q_finish(0, (nc.sync, nc.sync))
-        q_finish(1, (nc.sync, nc.scalar))
+        for t in range(2):
+            neg_max(z_max[t][:], z_ps[t][:])
+            nc.scalar.activation(out=p_exp[t][:], in_=z_ps[t][:], func=ACT.Exp, bias=z_max[t][:], accum_out=z_sum[t][:])
+        for t in range(2):
+            nc.vector.reciprocal(out=q_rec[t][:], in_=q_sum[t][:])
+            nc.vector.tensor_scalar(out=p_share[t][:], in0=q_exp[t][:], scalar1=q_rec[t][:], scalar2=-256.0, op0=ALU.mult, op1=ALU.mult)
+        for t in range(2):
+            nc.vector.reciprocal(out=z_rec[t][:], in_=z_sum[t][:])
+            nc.vector.tensor_scalar(out=q_fac[t][:], in0=z_rec[t][:], scalar1=256.0, scalar2=None, op0=ALU.mult)
+        for t in range(2):
+            for h in range(2):
+                cols = slice(h * HALF, (h + 1) * HALF)
+                nc.vector.scalar_tensor_tensor(out=res[t][h][:], in0=p_exp[t][:, cols], scalar=q_fac[t][:], in1=p_share[t][:, cols], op0=ALU.mult, op1=ALU.add)
+                (nc.scalar if h else nc.sync).dma_start(out=out[t * P : (t + 1) * P, cols], in_=res[t][h][:])

@@ -56,7 +56,7 @@ def tile_list_teacher_at_listed_classes_kernel(tc, xt_words, xt_scales, wc, xl_w
 
         def load_scales(eng, plane, src, quads):
             for q in quads:
-                eng.dma_start(out=plane[32 * q : 32 * q + 4].bitcast(I32), in_=src[:, 4 * q : 4 * q + 4, :].rearrange("z r n -> r z n").bitcast(I32))
+                eng.dma_start(out=plane[q:P:32].bitcast(I32), in_=src[:, q:16:4, :].rearrange("z r n -> r z n").bitcast(I32))
 
         def load_wc(h):
             nc.sync.dma_start(out=raw[h][:], in_=wc[:, h * HALF : (h + 1) * HALF].rearrange("(p t) j -> p t j", t=4))

@@ -18,139 +18,170 @@ ACT = mybir.ActivationFunctionType
 AX = mybir.AxisListType
 
 P = 128
-HALF = 256
-VCOLS = 176
+PACK = 4
+TILES = T // P
+PASSES = L // (P * PACK)
+BANK = 512
+HALF = J // 2
+GAIN = 256.0
+VECTOR_COLUMNS = 64
 
 
-def tile_list_teacher_at_listed_classes_kernel(tc, xt_words, xt_scales, wc, xl_words, xl_scales, wl_words, wl_scales, offs, out):
+def tile_list_teacher_at_listed_classes_kernel(
+    tc, xt_words, xt_scales, wc, xl_words, xl_scales, wl_words, wl_scales, offs, out
+):
     nc = tc.nc
     with ExitStack() as ctx:
         lists = ctx.enter_context(tc.tile_pool(name="lists", bufs=1))
         keep = ctx.enter_context(tc.tile_pool(name="keep", bufs=1))
         psum = ctx.enter_context(tc.psum_pool(name="psum", bufs=1))
 
+        def pair(name, shape, dtype, align=None):
+            return [keep.tile(shape, dtype, name="%s%d" % (name, i), align_bytes=align) for i in range(2)]
+
         offsets = lists.tile([P, J // 16], U16, name="offsets")
         xt_w = keep.tile([P, T], U32, name="xt_w", align_bytes=64)
-        xl_w = keep.tile([P, 2, 2 * T], U8, name="xl_w", align_bytes=64)
-        wl_w = [keep.tile([P, 2, 512], U32, name="wl_w%d" % h, align_bytes=64) for h in range(2)]
+        xl_w = keep.tile([P, PASSES, 2 * T], U8, name="xl_w", align_bytes=64)
+        wl_w = pair("wl_w", [P, PASSES, BANK], U32, 64)
         xt_s = keep.tile([P, 1, T], U8, name="xt_s", align_bytes=64)
-        xl_s = keep.tile([P, 2, T], U8, name="xl_s", align_bytes=64)
-        wl_s = keep.tile([P, 2, C], U8, name="wl_s", align_bytes=64)
-        raw = [keep.tile([P, 4, HALF], F32, name="raw%d" % h) for h in range(2)]
-        grouped = [keep.tile([P, HALF, 4], BF16, name="grouped%d" % h, align_bytes=64) for h in range(2)]
-        wc_w = [keep.tile([P, HALF], U32, name="wc_w%d" % h, align_bytes=64) for h in range(2)]
-        wc_s = [keep.tile([P, HALF], U8, name="wc_s%d" % h, align_bytes=64) for h in range(2)]
-        u_sb = [keep.tile([P, C], F32, name="u_sb%d" % t) for t in range(2)]
-        picked = [keep.tile([P, J], F32, name="picked%d" % t) for t in range(2)]
-        p_exp = [keep.tile([P, J], F32, name="p_exp%d" % t) for t in range(2)]
-        p_share = [keep.tile([P, J], F32, name="p_share%d" % t) for t in range(2)]
-        q_exp = [keep.tile([P, J], F32, name="q_exp%d" % t) for t in range(2)]
-        res = [[keep.tile([P, HALF], F32, name="res%d_%d" % (t, h)) for h in range(2)] for t in range(2)]
-        col = lambda name: [keep.tile([P, 1], F32, name="%s%d" % (name, t)) for t in range(2)]
-        z_max, z_sum, z_rec, q_max, q_sum, q_rec, q_fac = (col(n) for n in ("zm", "zs", "zr", "qm", "qs", "qr", "qf"))
-        z_sums = keep.tile([P, 2], F32, name="z_sums")
-        z_recs = keep.tile([P, 2], F32, name="z_recs")
-        z_facs = keep.tile([P, 2], F32, name="z_facs")
-        z_ps = [psum.tile([P, J], F32, name="z_ps%d" % t) for t in range(2)]
-        u_ps = [[psum.tile([P, 512], F32, name="u_ps%d_%d" % (t, h)) for h in range(2)] for t in range(2)]
+        xl_s = keep.tile([P, PASSES, T], U8, name="xl_s", align_bytes=64)
+        wl_s = keep.tile([P, PASSES, C], U8, name="wl_s", align_bytes=64)
+        raw = pair("raw", [P, PACK, HALF], F32)
+        grouped = pair("grouped", [P, HALF, PACK], BF16, 64)
+        wc_w = pair("wc_w", [P, HALF], U32, 64)
+        wc_s = pair("wc_s", [P, HALF], U8, 64)
+        u_sb = pair("u_sb", [P, C], F32)
+        picked = pair("picked", [P, J], F32)
+        p_exp = pair("p_exp", [P, J], F32)
+        q_term = pair("q_term", [P, J], F32)
+        q_exp = pair("q_exp", [P, J], F32)
+        result = [pair("result%d_" % t, [P, HALF], F32) for t in range(TILES)]
+        z_neg_max = pair("z_neg_max", [P, 1], F32)
+        p_sum = pair("p_sum", [P, 1], F32)
+        p_inverse = pair("p_inverse", [P, 1], F32)
+        p_factor = pair("p_factor", [P, 1], F32)
+        q_sum = keep.tile([P, TILES], F32, name="q_sum")
+        q_inverse = keep.tile([P, TILES], F32, name="q_inverse")
+        z_ps = [psum.tile([P, J], F32, name="z_ps%d" % t) for t in range(TILES)]
+        u_low = psum.tile([P, BANK], F32, name="u_low")
+        u_ps = [[u_low, psum.tile([P, BANK], F32, name="u_high%d" % t)] for t in range(TILES)]
 
-        def load_scales(eng, plane, src, quads):
-            for q in quads:
-                eng.dma_start(out=plane[q:P:32].bitcast(I32), in_=src[:, q:16:4, :].rearrange("z r n -> r z n").bitcast(I32))
+        def load_scales(engine, plane, scales, rows):
+            for r in rows:
+                engine.dma_start(
+                    out=plane[r:P:32].bitcast(I32),
+                    in_=scales[:, r:16:4, :].rearrange("z q n -> q z n").bitcast(I32),
+                )
 
         def load_wc(h):
-            nc.sync.dma_start(out=raw[h][:], in_=wc[:, h * HALF : (h + 1) * HALF].rearrange("(p t) j -> p t j", t=4))
+            columns = wc[:, h * HALF : (h + 1) * HALF]
+            nc.sync.dma_start(out=raw[h][:], in_=columns.rearrange("(p t) j -> p t j", t=PACK))
 
         def load_wl(h):
-            nc.sync.dma_start(out=wl_w[h][:].bitcast(I32), in_=wl_words[:, :, 512 * h : 512 * h + 512, :].rearrange("z p n t -> p z (n t)").bitcast(I32))
+            columns = wl_words[:, :, h * BANK : (h + 1) * BANK, :]
+            nc.sync.dma_start(out=wl_w[h][:].bitcast(I32), in_=columns.rearrange("z p n t -> p z (n t)").bitcast(I32))
 
-        def interleave(h, split):
-            for eng, a, b in ((nc.vector, 0, split), (nc.scalar, split, HALF)):
-                if a == b:
-                    continue
-                dst = grouped[h][:, a:b, :].rearrange("p (c i) t -> p c t i", i=4)
-                src = raw[h][:, :, a:b].rearrange("p t (c i) -> p c t i", i=4)
-                if eng is nc.vector:
-                    eng.tensor_copy(out=dst, in_=src)
-                else:
-                    eng.activation(out=dst, in_=src, func=ACT.Copy)
+        def interleaving_views(h, first, last):
+            dst = grouped[h][:, first:last, :].rearrange("p (c i) t -> p c t i", i=4)
+            src = raw[h][:, :, first:last].rearrange("p t (c i) -> p c t i", i=4)
+            return dst, src
 
         def quantise(h):
-            nc.vector.quantize_mx(out=wc_w[h][:].bitcast(FP8X4), scales=wc_s[h][:], in_=grouped[h][:].rearrange("p c t -> p (c t)"))
+            nc.vector.quantize_mx(
+                out=wc_w[h][:].bitcast(FP8X4), scales=wc_s[h][:], in_=grouped[h][:].rearrange("p c t -> p (c t)")
+            )
 
-        def student_mm(h):
-            for t in range(2):
-                nc.tensor.matmul_mx(out=z_ps[t][:, h * HALF : (h + 1) * HALF], lhsT=xt_w[:, t * P : (t + 1) * P].bitcast(FP8X4), lhsT_scale=xt_s[:, 0, t * P : (t + 1) * P], rhs=wc_w[h][:].bitcast(FP8X4), rhs_scale=wc_s[h][:], start=True, stop=True)
-
-        def teacher_mm(t, h):
-            for z in range(2):
-                nc.tensor.matmul_mx(out=u_ps[t][h][:], lhsT=xl_w[:, z, 2 * t * P : 2 * (t + 1) * P].bitcast(FP4X4), lhsT_scale=xl_s[:, z, t * P : (t + 1) * P], rhs=wl_w[h][:, z, :].bitcast(FP8X4), rhs_scale=wl_s[:, z, 512 * h : 512 * h + 512], start=(z == 0), stop=(z == 1))
-
-        def evac(t, h):
-            nc.scalar.activation(out=u_sb[t][:, 512 * h : 512 * h + 512], in_=u_ps[t][h][:], func=ACT.Copy)
-
-        def neg_max(dst, src):
+        def negated_row_max(dst, src):
             nc.vector.tensor_reduce(out=dst, in_=src, axis=AX.X, op=ALU.max, negate=True)
 
         def gather(t):
             nc.vector.tensor_copy(out=picked[t][:], in_=u_sb[t][:].indirect(offsets[:]))
 
-        def q_finish(t, engs):
-            nc.vector.reciprocal(out=q_rec[t][:], in_=q_sum[t][:])
-            nc.vector.tensor_scalar(out=q_fac[t][:], in0=q_rec[t][:], scalar1=-256.0, scalar2=None, op0=ALU.mult)
-            for h in range(2):
-                cols = slice(h * HALF, (h + 1) * HALF)
-                nc.vector.scalar_tensor_tensor(out=res[t][h][:], in0=q_exp[t][:, cols], scalar=q_fac[t][:], in1=p_share[t][:, cols], op0=ALU.mult, op1=ALU.add)
-                engs[h].dma_start(out=out[t * P : (t + 1) * P, cols], in_=res[t][h][:])
-
-        load_scales(nc.sync, xl_s, xl_scales, (0,))
-        load_scales(nc.scalar, xl_s, xl_scales, (1,))
-        load_scales(nc.sync, xl_s, xl_scales, (2,))
-        load_scales(nc.scalar, xl_s, xl_scales, (3,))
+        for r in range(4):
+            load_scales(nc.scalar if r % 2 else nc.sync, xl_s, xl_scales, (r,))
         load_scales(nc.scalar, wl_s, wl_scales, (0, 1))
         nc.sync.dma_start(out=xl_w[:].bitcast(I32), in_=xl_words.rearrange("z p b -> p z b").bitcast(I32))
         load_wl(0)
         load_scales(nc.sync, wl_s, wl_scales, (2, 3))
         load_wl(1)
         nc.sync.dma_start(offsets[:], offs)
-        load_scales(nc.scalar, xt_s, xt_scales, (0, 1))
         load_wc(0)
         load_wc(1)
-        load_scales(nc.sync, xt_s, xt_scales, (2, 3))
+        load_scales(nc.sync, xt_s, xt_scales, range(4))
         nc.sync.dma_start(out=xt_w[:].bitcast(I32), in_=xt_words[0].rearrange("p n t -> p (n t)").bitcast(I32))
-        u_ps[1][0] = u_ps[0][0]
-        teacher_mm(0, 0)
-        teacher_mm(0, 1)
-        evac(0, 0)
-        evac(0, 1)
-        teacher_mm(1, 0)
-        teacher_mm(1, 1)
-        evac(1, 0)
-        evac(1, 1)
-        interleave(0, HALF)
+
+        for t in range(TILES):
+            for h in range(2):
+                for z in range(PASSES):
+                    nc.tensor.matmul_mx(
+                        out=u_ps[t][h][:],
+                        lhsT=xl_w[:, z, 2 * t * P : 2 * (t + 1) * P].bitcast(FP4X4),
+                        lhsT_scale=xl_s[:, z, t * P : (t + 1) * P],
+                        rhs=wl_w[h][:, z, :].bitcast(FP8X4),
+                        rhs_scale=wl_s[:, z, h * BANK : (h + 1) * BANK],
+                        start=(z == 0),
+                        stop=(z == PASSES - 1),
+                    )
+            for h in range(2):
+                nc.scalar.activation(out=u_sb[t][:, h * BANK : (h + 1) * BANK], in_=u_ps[t][h][:], func=ACT.Copy)
+
+        dst, src = interleaving_views(0, 0, HALF)
+        nc.vector.tensor_copy(out=dst, in_=src)
         gather(0)
         quantise(0)
-        interleave(1, 0)
+        dst, src = interleaving_views(1, 0, VECTOR_COLUMNS)
+        nc.vector.tensor_copy(out=dst, in_=src)
+        dst, src = interleaving_views(1, VECTOR_COLUMNS, HALF)
+        nc.scalar.activation(out=dst, in_=src, func=ACT.Copy)
         gather(1)
         quantise(1)
-        student_mm(0)
-        student_mm(1)
-        spent = grouped[1][:].rearrange("p c t -> p (c t)").bitcast(F32)
-        q_neg = [spent[:, 8 * t : 8 * t + 1] for t in range(2)]
-        for t in range(2):
-            neg_max(q_neg[t], picked[t][:])
-            nc.scalar.activation(out=q_exp[t][:], in_=picked[t][:], func=ACT.Exp, bias=q_neg[t], accum_out=q_sum[t][:])
-        for t in range(2):
-            neg_max(z_max[t][:], z_ps[t][:])
-            nc.scalar.activation(out=p_exp[t][:], in_=z_ps[t][:], func=ACT.Exp, bias=z_max[t][:], accum_out=z_sum[t][:])
-        for t in range(2):
-            nc.vector.reciprocal(out=q_rec[t][:], in_=q_sum[t][:])
-            nc.vector.tensor_scalar(out=p_share[t][:], in0=q_exp[t][:], scalar1=q_rec[t][:], scalar2=-256.0, op0=ALU.mult, op1=ALU.mult)
-        for t in range(2):
-            nc.vector.reciprocal(out=z_rec[t][:], in_=z_sum[t][:])
-            nc.vector.tensor_scalar(out=q_fac[t][:], in0=z_rec[t][:], scalar1=256.0, scalar2=None, op0=ALU.mult)
-        for t in range(2):
+
+        for h in range(2):
+            for t in range(TILES):
+                nc.tensor.matmul_mx(
+                    out=z_ps[t][:, h * HALF : (h + 1) * HALF],
+                    lhsT=xt_w[:, t * P : (t + 1) * P].bitcast(FP8X4),
+                    lhsT_scale=xt_s[:, 0, t * P : (t + 1) * P],
+                    rhs=wc_w[h][:].bitcast(FP8X4),
+                    rhs_scale=wc_s[h][:],
+                    start=True,
+                    stop=True,
+                )
+
+        for t in range(TILES):
+            q_neg_max = raw[1][:, t, HALF - 1 : HALF]
+            negated_row_max(q_neg_max, picked[t][:])
+            nc.scalar.activation(
+                out=q_exp[t][:], in_=picked[t][:], func=ACT.Exp, bias=q_neg_max, accum_out=q_sum[:, t : t + 1]
+            )
+        for t in range(TILES):
+            negated_row_max(z_neg_max[t][:], z_ps[t][:])
+            nc.scalar.activation(
+                out=p_exp[t][:], in_=z_ps[t][:], func=ACT.Exp, bias=z_neg_max[t][:], accum_out=p_sum[t][:]
+            )
+
+        nc.vector.reciprocal(out=q_inverse[:], in_=q_sum[:])
+        for t in range(TILES):
+            nc.vector.tensor_scalar(
+                out=q_term[t][:],
+                in0=q_exp[t][:],
+                scalar1=q_inverse[:, t : t + 1],
+                scalar2=-GAIN,
+                op0=ALU.mult,
+                op1=ALU.mult,
+            )
+        for t in range(TILES):
+            nc.vector.reciprocal(out=p_inverse[t][:], in_=p_sum[t][:])
+            nc.vector.tensor_scalar(out=p_factor[t][:], in0=p_inverse[t][:], scalar1=GAIN, scalar2=None, op0=ALU.mult)
+        for t in range(TILES):
             for h in range(2):
-                cols = slice(h * HALF, (h + 1) * HALF)
-                nc.vector.scalar_tensor_tensor(out=res[t][h][:], in0=p_exp[t][:, cols], scalar=q_fac[t][:], in1=p_share[t][:, cols], op0=ALU.mult, op1=ALU.add)
-                (nc.scalar if h else nc.sync).dma_start(out=out[t * P : (t + 1) * P, cols], in_=res[t][h][:])
+                slots = slice(h * HALF, (h + 1) * HALF)
+                nc.vector.scalar_tensor_tensor(
+                    out=result[t][h][:],
+                    in0=p_exp[t][:, slots],
+                    scalar=p_factor[t][:],
+                    in1=q_term[t][:, slots],
+                    op0=ALU.mult,
+                    op1=ALU.add,
+                )
+                (nc.scalar if h else nc.sync).dma_start(out=out[t * P : (t + 1) * P, slots], in_=result[t][h][:])

from contextlib import ExitStack

import concourse.mybir as mybir

K, L, T, C, J = 512, 1024, 256, 1024, 512
FLOPS = 2 * T * (K * J + L * C)

F32 = mybir.dt.float32
BF16 = mybir.dt.bfloat16
I32 = mybir.dt.int32
U32 = mybir.dt.uint32
U16 = mybir.dt.uint16
U8 = mybir.dt.uint8
FP8X4 = mybir.dt.float8_e4m3fn_x4
FP4X4 = mybir.dt.float4_e2m1fn_x4
ALU = mybir.AluOpType
ACT = mybir.ActivationFunctionType
AX = mybir.AxisListType

P = 128
PACK = 4
TILES = T // P
PASSES = L // (P * PACK)
BANK = 512
HALF = J // 2
GAIN = 256.0
VECTOR_COLUMNS = 64


def tile_list_teacher_at_listed_classes_kernel(
    tc, xt_words, xt_scales, wc, xl_words, xl_scales, wl_words, wl_scales, offs, out
):
    nc = tc.nc
    with ExitStack() as ctx:
        lists = ctx.enter_context(tc.tile_pool(name="lists", bufs=1))
        keep = ctx.enter_context(tc.tile_pool(name="keep", bufs=1))
        psum = ctx.enter_context(tc.psum_pool(name="psum", bufs=1))

        def pair(name, shape, dtype, align=None):
            return [keep.tile(shape, dtype, name="%s%d" % (name, i), align_bytes=align) for i in range(2)]

        offsets = lists.tile([P, J // 16], U16, name="offsets")
        xt_w = keep.tile([P, T], U32, name="xt_w", align_bytes=64)
        xl_w = keep.tile([P, PASSES, 2 * T], U8, name="xl_w", align_bytes=64)
        wl_w = pair("wl_w", [P, PASSES, BANK], U32, 64)
        xt_s = keep.tile([P, 1, T], U8, name="xt_s", align_bytes=64)
        xl_s = keep.tile([P, PASSES, T], U8, name="xl_s", align_bytes=64)
        wl_s = keep.tile([P, PASSES, C], U8, name="wl_s", align_bytes=64)
        raw = pair("raw", [P, PACK, HALF], F32)
        grouped = pair("grouped", [P, HALF, PACK], BF16, 64)
        wc_w = pair("wc_w", [P, HALF], U32, 64)
        wc_s = pair("wc_s", [P, HALF], U8, 64)
        u_sb = pair("u_sb", [P, C], F32)
        picked = pair("picked", [P, J], F32)
        p_exp = pair("p_exp", [P, J], F32)
        q_term = pair("q_term", [P, J], F32)
        q_exp = pair("q_exp", [P, J], F32)
        result = [pair("result%d_" % t, [P, HALF], F32) for t in range(TILES)]
        z_neg_max = pair("z_neg_max", [P, 1], F32)
        p_sum = pair("p_sum", [P, 1], F32)
        p_inverse = pair("p_inverse", [P, 1], F32)
        p_factor = pair("p_factor", [P, 1], F32)
        q_sum = keep.tile([P, TILES], F32, name="q_sum")
        q_inverse = keep.tile([P, TILES], F32, name="q_inverse")
        z_ps = [psum.tile([P, J], F32, name="z_ps%d" % t) for t in range(TILES)]
        u_low = psum.tile([P, BANK], F32, name="u_low")
        u_ps = [[u_low, psum.tile([P, BANK], F32, name="u_high%d" % t)] for t in range(TILES)]

        def load_scales(engine, plane, scales, rows):
            for r in rows:
                engine.dma_start(
                    out=plane[r:P:32].bitcast(I32),
                    in_=scales[:, r:16:4, :].rearrange("z q n -> q z n").bitcast(I32),
                )

        def load_wc(h):
            columns = wc[:, h * HALF : (h + 1) * HALF]
            nc.sync.dma_start(out=raw[h][:], in_=columns.rearrange("(p t) j -> p t j", t=PACK))

        def load_wl(h):
            columns = wl_words[:, :, h * BANK : (h + 1) * BANK, :]
            nc.sync.dma_start(out=wl_w[h][:].bitcast(I32), in_=columns.rearrange("z p n t -> p z (n t)").bitcast(I32))

        def interleaving_views(h, first, last):
            dst = grouped[h][:, first:last, :].rearrange("p (c i) t -> p c t i", i=4)
            src = raw[h][:, :, first:last].rearrange("p t (c i) -> p c t i", i=4)
            return dst, src

        def quantise(h):
            nc.vector.quantize_mx(
                out=wc_w[h][:].bitcast(FP8X4), scales=wc_s[h][:], in_=grouped[h][:].rearrange("p c t -> p (c t)")
            )

        def negated_row_max(dst, src):
            nc.vector.tensor_reduce(out=dst, in_=src, axis=AX.X, op=ALU.max, negate=True)

        def gather(t):
            nc.vector.tensor_copy(out=picked[t][:], in_=u_sb[t][:].indirect(offsets[:]))

        for r in range(4):
            load_scales(nc.scalar if r % 2 else nc.sync, xl_s, xl_scales, (r,))
        load_scales(nc.scalar, wl_s, wl_scales, (0, 1))
        nc.sync.dma_start(out=xl_w[:].bitcast(I32), in_=xl_words.rearrange("z p b -> p z b").bitcast(I32))
        load_wl(0)
        load_scales(nc.sync, wl_s, wl_scales, (2, 3))
        load_wl(1)
        nc.sync.dma_start(offsets[:], offs)
        load_wc(0)
        load_wc(1)
        load_scales(nc.sync, xt_s, xt_scales, range(4))
        nc.sync.dma_start(out=xt_w[:].bitcast(I32), in_=xt_words[0].rearrange("p n t -> p (n t)").bitcast(I32))

        for t in range(TILES):
            for h in range(2):
                for z in range(PASSES):
                    nc.tensor.matmul_mx(
                        out=u_ps[t][h][:],
                        lhsT=xl_w[:, z, 2 * t * P : 2 * (t + 1) * P].bitcast(FP4X4),
                        lhsT_scale=xl_s[:, z, t * P : (t + 1) * P],
                        rhs=wl_w[h][:, z, :].bitcast(FP8X4),
                        rhs_scale=wl_s[:, z, h * BANK : (h + 1) * BANK],
                        start=(z == 0),
                        stop=(z == PASSES - 1),
                    )
            for h in range(2):
                nc.scalar.activation(out=u_sb[t][:, h * BANK : (h + 1) * BANK], in_=u_ps[t][h][:], func=ACT.Copy)

        dst, src = interleaving_views(0, 0, HALF)
        nc.vector.tensor_copy(out=dst, in_=src)
        gather(0)
        quantise(0)
        dst, src = interleaving_views(1, 0, VECTOR_COLUMNS)
        nc.vector.tensor_copy(out=dst, in_=src)
        dst, src = interleaving_views(1, VECTOR_COLUMNS, HALF)
        nc.scalar.activation(out=dst, in_=src, func=ACT.Copy)
        gather(1)
        quantise(1)

        for h in range(2):
            for t in range(TILES):
                nc.tensor.matmul_mx(
                    out=z_ps[t][:, h * HALF : (h + 1) * HALF],
                    lhsT=xt_w[:, t * P : (t + 1) * P].bitcast(FP8X4),
                    lhsT_scale=xt_s[:, 0, t * P : (t + 1) * P],
                    rhs=wc_w[h][:].bitcast(FP8X4),
                    rhs_scale=wc_s[h][:],
                    start=True,
                    stop=True,
                )

        for t in range(TILES):
            q_neg_max = raw[1][:, t, HALF - 1 : HALF]
            negated_row_max(q_neg_max, picked[t][:])
            nc.scalar.activation(
                out=q_exp[t][:], in_=picked[t][:], func=ACT.Exp, bias=q_neg_max, accum_out=q_sum[:, t : t + 1]
            )
        for t in range(TILES):
            negated_row_max(z_neg_max[t][:], z_ps[t][:])
            nc.scalar.activation(
                out=p_exp[t][:], in_=z_ps[t][:], func=ACT.Exp, bias=z_neg_max[t][:], accum_out=p_sum[t][:]
            )

        nc.vector.reciprocal(out=q_inverse[:], in_=q_sum[:])
        for t in range(TILES):
            nc.vector.tensor_scalar(
                out=q_term[t][:],
                in0=q_exp[t][:],
                scalar1=q_inverse[:, t : t + 1],
                scalar2=-GAIN,
                op0=ALU.mult,
                op1=ALU.mult,
            )
        for t in range(TILES):
            nc.vector.reciprocal(out=p_inverse[t][:], in_=p_sum[t][:])
            nc.vector.tensor_scalar(out=p_factor[t][:], in0=p_inverse[t][:], scalar1=GAIN, scalar2=None, op0=ALU.mult)
        for t in range(TILES):
            for h in range(2):
                slots = slice(h * HALF, (h + 1) * HALF)
                nc.vector.scalar_tensor_tensor(
                    out=result[t][h][:],
                    in0=p_exp[t][:, slots],
                    scalar=p_factor[t][:],
                    in1=q_term[t][:, slots],
                    op0=ALU.mult,
                    op1=ALU.add,
                )
                (nc.scalar if h else nc.sync).dma_start(out=out[t * P : (t + 1) * P, slots], in_=result[t][h][:])
